import numpy as np, ml_dtypes
CORES = [2,3,42,43,82,83,122,123]
N = 8
BF = ml_dtypes.bfloat16
def f(rng, *shape):
    return (rng.standard_normal(shape, dtype=np.float32) * np.exp2(rng.integers(-2, 3, shape[:-1] + (1,)))).astype(BF)
def wide(rng, *shape):
    v = f(rng, *shape).astype(np.float32); k = shape[:-2] + (1, shape[-1])
    return (v * np.exp2(rng.integers(-6, 7, k)) * (rng.random(k) > 0.0625)).astype(BF)
def gentries(a):
    return np.ascontiguousarray(a.reshape(8, 16, -1).transpose(0, 2, 1)).reshape(8, -1)
def gtable(e):
    e = np.asarray(e); return np.ascontiguousarray(e.reshape(8, -1, 16).transpose(0, 2, 1)).reshape(128, -1).astype(np.int32)
D, V, S, CL, W, B, M = 3, 2048, 256, 4, 2, 64, 512
def places(rng):
    v = rng.standard_normal((N, 8, 1, D * V), dtype=np.float32) + 0.5 * rng.standard_normal((N, 8, 16, D * V), dtype=np.float32)
    return (v * np.exp2(rng.integers(-1, 2, (N, 8, 1, 1)))).astype(BF).reshape(N, 128, D * V)
def draw(rng):
    e = np.argsort(rng.random((N, 8, CL, V)), -1)[..., :2 * S].reshape(N, 8, CL, 2, S)
    b = np.argsort(rng.random((N, 8, V)), -1)[..., :N * B].reshape(N, 8, N, B)
    return e, b, rng.integers(0, V, (N, 8, M))
def both(s):
    k = np.arange(N); return np.where(k[:, None, None, None] > k[None, None, :, None], s, s.transpose(2, 1, 0, 3))
def net(rng, pos, e, b, w):
    x = pos.astype(np.float32).reshape(N, 8, 16, D, V); own = np.zeros((N, 8, CL, S)); jo = np.zeros((N, 8, N, B))
    for r in range(N):
        for g in range(8):
            v = x[r, g][..., e[r, g]]; own[r, g] = np.mean(np.sum(np.square(v[..., 0, :] - v[..., 1, :]), 1), 0)
            for q in range(r):
                u = x[r, g][..., b[r, g, q]] - x[q, g][..., b[q, g, r]]
                jo[r, g, q] = np.mean(np.sum(np.square(u), 1), 0); jo[q, g, r] = jo[r, g, q]
    def stiffness(*shape):
        return rng.random(shape) * 0.375 * (rng.random(shape) > 0.03125)
    def inverse(m, t, z):
        return np.minimum(np.exp2(t - np.log2(m + 2.0 ** -12)), 4096) * (z > 0.03125)
    k = stiffness(N, 8, CL, S); h = inverse(own, rng.uniform(-2, 2, own.shape), rng.random(own.shape))
    kj = both(stiffness(N, 8, N, B)); hj = inverse(jo, both(rng.uniform(-2, 2, jo.shape)), both(rng.random(jo.shape)))
    return {"pos": pos, "ends": np.stack([gtable(a.reshape(8, -1)) for a in e]), "stiff": k.astype(BF).reshape(N, 8, CL * S), "inv": h.astype(BF).reshape(N, 8, CL * S),
            "bord": np.stack([gtable(a.reshape(8, -1)) for a in b]), "jstiff": kj.astype(BF).reshape(N, 8, N * B), "jinv": hj.astype(BF).reshape(N, 8, N * B), "watch": np.stack([gtable(a) for a in w])}
def setup_inputs(rng):
    return net(rng, places(rng), *draw(rng))
def setup_inputs_again(rng):
    H = max(2 * S, N * B); hub = np.argsort(rng.random((N, 8, V)), -1)[..., :H]
    e = np.take_along_axis(np.repeat(hub[:, :, None], CL, 2), np.argsort(rng.random((N, 8, CL, H)), -1)[..., :2 * S], -1).reshape(N, 8, CL, 2, S)
    b = np.take_along_axis(hub, np.argsort(rng.random((N, 8, H)), -1)[..., :N * B], -1).reshape(N, 8, N, B)
    return net(rng, places(rng), e, b, np.take_along_axis(hub, rng.integers(0, H, (N, 8, M)), -1))
def setup_inputs_ends(rng):
    e, b, w = draw(rng); s = np.arange(S); w = rng.integers(0, 2 * S, (N, 8, M))
    for c in range(CL):
        e[:, :, c, 0] = 2 * s + c; e[:, :, c, 1] = 2 * s + 1 + c
    b[:] = np.arange(N * B).reshape(N, B); w[:, :, 0] = 0
    for a in (e, b, w):
        a[:, 1::2] = V - 1 - a[:, 1::2]
    w[:, 0::2, -1] = V - 1; w[:, 1::2, -1] = 0
    return net(rng, places(rng), e, b, w)
def setup_inputs_still(rng):
    d = net(rng, rng.integers(-1, 2, (N, 128, D * V)).astype(np.float32).astype(BF), *draw(rng))
    ks = np.array([0, 0.125, 0.25, 0.375]); hs = np.array([0, 0.125, 0.25, 0.5, 1, 2])
    d["stiff"] = rng.choice(ks, (N, 8, CL * S)).astype(BF); d["inv"] = rng.choice(hs, (N, 8, CL * S)).astype(BF)
    d["jstiff"] = both(rng.choice(ks, (N, 8, N, B))).astype(BF).reshape(N, 8, N * B); d["jinv"] = both(rng.choice(hs, (N, 8, N, B))).astype(BF).reshape(N, 8, N * B)
    return d
def setup_inputs_border(rng):
    e, b, w = draw(rng); w = np.take_along_axis(b.reshape(N, 8, N * B), rng.integers(0, N * B, (N, 8, M)), -1)
    d = net(rng, places(rng), e, b, w); d["stiff"] = np.zeros((N, 8, CL * S), np.float32).astype(BF); return d
def setup_inputs_spread(rng):
    return net(rng, wide(rng, N, 128, D * V), *draw(rng))
def differ(a):
    s = np.sort(a, -1); return bool((s[..., 1:] != s[..., :-1]).all())
def check_inputs(d):
    bad = []; e, b, w = [np.stack([gentries(a) for a in d[n]]) for n in ("ends", "bord", "watch")]
    for n, a in (("ends", e), ("bord", b), ("watch", w)):
        if a.min() < 0 or a.max() >= V: bad.append(n + ": not a vertex")
    if not differ(e.reshape(N, 8, CL, 2 * S)): bad.append("a vertex twice in a class")
    if not differ(b.reshape(N, 8, N * B)): bad.append("a vertex twice in bord")
    if not (np.abs(d["pos"].astype(np.float32)) <= 8192).all(): bad.append("pos")
    for n, top in (("stiff", 0.375), ("jstiff", 0.375), ("inv", 4096), ("jinv", 4096)):
        a = d[n].astype(np.float32)
        if not ((a >= 0) & (a <= top)).all(): bad.append(n)
    for n in ("jstiff", "jinv"):
        a = d[n].astype(np.float32).reshape(N, 8, N, B)
        if not (a == a.transpose(2, 1, 0, 3)).all(): bad.append(n + ": not alike on both sides")
    return bad
def push(d, k, w):
    q = np.sum(d * d, 1, keepdims=True)
    return np.minimum(np.maximum(k * (1 - w * q), -0.25), 0.25) * d
def reference(pos, ends, stiff, inv, bord, jstiff, jinv, watch):
    x = pos.astype(np.float64).reshape(N, 8, 16, D, V)
    e = np.stack([gentries(a) for a in ends]).reshape(N, 8, CL, 2, S); b = np.stack([gentries(a) for a in bord]).reshape(N, 8, N, B); v = np.stack([gentries(a) for a in watch])
    k = stiff.astype(np.float64).reshape(N, 8, CL, S); w = inv.astype(np.float64).reshape(N, 8, CL, S)
    kj = jstiff.astype(np.float64).reshape(N, 8, N, B); wj = jinv.astype(np.float64).reshape(N, 8, N, B)
    for t in range(W):
        for c in range(CL):
            for r in range(N):
                for g in range(8):
                    i, j = e[r, g, c]; z = x[r, g]; m = push(z[..., i] - z[..., j], k[r, g, c], w[r, g, c])
                    z[..., i] += m; z[..., j] -= m
        h = np.stack([np.stack([x[r, g][..., b[r, g]] for g in range(8)]) for r in range(N)])
        for r in range(N):
            for g in range(8):
                d = h[r, g] - h[:, g, :, :, r].transpose(1, 2, 0, 3); z = x[r, g]
                z[..., b[r, g]] += push(d, kj[r, g], wj[r, g])
    y = np.stack([np.stack([x[r, g][..., v[r, g]] for g in range(8)]) for r in range(N)])
    return {"y": y.reshape(N, 128, D * M).astype(np.float32)}

from concourse.bass import DstId, RemoteDMATransfer
from concourse.mybir import AluOpType, ActivationFunctionType

N, D, V, S, CL, B, M = 8, 3, 2048, 256, 4, 64, 512
J = (N - 1) * B
PAD = 32
RJ = PAD + CL * 2 * S
BASE = RJ + J
WW = BASE + V
NS = CL * S + J

SCRATCH = {
    "win0": ("sbuf", [128, WW], "float32"), "win1": ("sbuf", [128, WW], "float32"), "win2": ("sbuf", [128, WW], "float32"),
    "posb": ("sbuf", [128, D * V], "bfloat16"),
    "loc": ("sbuf", [128, V], "float32"),
    "fac": ("sbuf", [128, 3 * NS], "float32"), "slot": ("sbuf", [128, 3 * NS], "float32"),
    "rb": ("sbuf", [128, 5 * 512], "float32"),
    "val": ("sbuf", [128, 4 * 512], "float32"),
    "snd0": ("sbuf", [128, D * J], "float32"), "snd1": ("sbuf", [128, D * J], "float32"),
    "land0": ("sbuf", [128, D * J], "float32"), "land1": ("sbuf", [128, D * J], "float32"),
    "yb": ("sbuf", [128, D * M], "float32"),
    "zb": ("sbuf", [128, D * S], "float32"), "xb": ("sbuf", [128, D * S], "float32"),
    "db": ("sbuf", [128, D * J], "float32"), "mb": ("sbuf", [128, D * J], "float32"),
    "sq1": ("sbuf", [128, J], "float32"), "ub": ("sbuf", [128, 3 * J], "float32"),
    "tabi": ("sbuf", [128, 192], "int32"), "tabf": ("sbuf", [128, 224], "float32"), "tt": ("sbuf", [128, 416], "float32"),
    "ul": ("sbuf", [128, 160], "uint16"), "ll": ("sbuf", [128, 192], "uint16"), "cl": ("sbuf", [128, 16], "uint16"),
    "ls": ("sbuf", [128, 320], "uint16"),
    "wraw": ("sbuf", [128, 288], "float32"), "wmin": ("sbuf", [128, 320], "float32"),
    "pi": ("sbuf", [128, 8], "int32"), "pj": ("sbuf", [128, 8], "int32"), "pf": ("sbuf", [128, 8], "float32"),
    "coli": ("sbuf", [128, 16], "float32"), "colj": ("sbuf", [128, 64], "float32"),
    "kk": ("sbuf", [128, 3072], "bfloat16"), "sel": ("sbuf", [128, 256], "bfloat16"),
    "pa": ("psum", [128, 512], "float32"), "pb": ("psum", [128, 512], "float32"), "pc": ("psum", [128, 512], "float32"),
    "p3": ("psum", [128, 512], "float32"), "p4": ("psum", [128, 512], "float32"),
    "px0": ("psum", [128, 512], "float32"), "px1": ("psum", [128, 512], "float32"), "px2": ("psum", [128, 512], "float32"),
}
POOLS = {"v": 30, "a": 30, "t": 20, "g": 28, "h": 26, "s": 4}
SEMAPHORES = [q + str(i) for q in POOLS for i in range(POOLS[q])] + ["arr%d" % i for i in range(6)] + ["sent", "swap", "left"]

CONV = ("g", "dma", "dma")
STRICT = False
COARSE = False
GP = ["C1", "f0", "C2", "v1", "C0", "f1", "v2", "f2", "v3", "f3", "swap", "j"]
PRE = ["fill", "U", "S0a", "const", "tab", "L", "R1a", "Z0v", "Z1v", "k0", "kw0", "Z2a"]
PLAN = {
    (0, "a1"): ["k1", "S1a", "R2a"], (0, "v3"): ["M1"], (0, "v4"): ["N1"],
    (1, "v0"): ["kw1"], (1, "a0"): ["k2"], (1, "a1"): ["S2a", "R3a"], (1, "v1"): ["M2"], (1, "v2"): ["N2"], (1, "v3"): ["kw2"],
    (2, "a0"): ["k3"], (2, "a1"): ["S3a"], (2, "v1"): ["M3"], (2, "v2"): ["N3"],
    (3, "v0"): ["kw3"], (3, "a0"): ["R4a"], (3, "a1"): ["k4"], (3, "v1"): ["UJ"], (3, "v3"): ["M4"], (3, "v4"): ["N4"],
    (4, "s"): ["S4v"], (4, "k"): ["kw4", "r0v", "r1a"],
    ((4, 0), "a0"): ["r2a", "r3a"], ((4, 1), "a0"): ["r4a"], ((4, 1), "v1"): ["m0"], ((4, 1), "v2"): ["n0"],
    (5, "v1"): ["m1"], (5, "v2"): ["n1"], (6, "v0"): ["cj"], (6, "v1"): ["mj"], (6, "v2"): ["nj"],
    (7, "v1"): ["mw"], (7, "v2"): ["nw"],
}


def peer_order(T, topo, r):
    chips = []
    for c in T.cores:
        if topo.chip(c) not in chips:
            chips.append(topo.chip(c))
    a = chips.index(topo.chip(T.cores[r]))
    others = sorted([b for b in range(len(chips)) if b != a], key=lambda b: (not topo.same_plane(chips[a], chips[b]), a ^ b))
    parts = [[q for q in range(N) if topo.chip(T.cores[q]) == chips[b]] for b in others]
    parts[0] = [q for q in range(N) if q != r and topo.chip(T.cores[q]) == chips[a]] + parts[0]
    return parts


def rank_program(g, core, T, topo):
    rank = T.rank_of(core)
    if rank is None:
        return
    A, F = AluOpType, ActivationFunctionType
    eng = {"v": g.vector, "a": g.scalar, "t": g.tensor, "g": g, "y": g.sync}
    ops, acc, bank, masks = [], {}, {}, {}

    def vw(name, a, b, s=1, rows=None):
        key = (a, b, 1 if COARSE else s)
        if key not in masks:
            masks[key] = ((1 << (b - a)) - 1) << a if key[2] == 1 else sum(1 << i for i in range(a, b, s))
        t = T[name]
        rs = slice(None) if rows is None else rows
        return (t[rs, a:b] if s == 1 else t[rs, a:b:s], [(name, masks[key])])

    def ind(win, off):
        return (win[0].indirect(off[0]), win[1], off[1])

    def op(q, fn, outs, ins, kind="c", sem=None):
        i, deps = len(ops), set()
        rd = [x for v in ins for part in v[1:] for x in part] + [x for v in outs for part in v[2:] for x in part]
        wr = [x for v in outs for x in v[1]]
        for lst, w in ((rd, False), (wr, True)):
            for name, m in lst:
                for (j, jw, jm) in acc.setdefault(name, []):
                    if jm & m and (w or jw) and j != i:
                        if w and not STRICT and kind == "c" and ops[j]["kind"] == "c" and ops[j]["q"] == q:
                            continue
                        deps.add(j)
                acc[name].append((i, w, m))
                if SCRATCH[name][0] == "psum":
                    deps.update(j for (j, jq) in bank.setdefault(name, []) if jq != q)
                    bank[name].append((i, q))
        ops.append({"q": q, "fn": fn, "deps": deps, "kind": kind, "sem": sem})

    def tt(o, x, y, f):
        op("v", lambda: g.vector.tensor_tensor(o[0], x[0], y[0], f), [o], [x, y])

    def ts(o, x, s1, s2, f0, f1=None):
        ins = [x] + [s for s in (s1, s2) if isinstance(s, tuple)]
        a1 = s1[0] if isinstance(s1, tuple) else s1
        a2 = s2[0] if isinstance(s2, tuple) else s2
        if f1 is None:
            op("v", lambda: g.vector.tensor_scalar(o[0], x[0], a1, None, f0), [o], ins)
        else:
            op("v", lambda: g.vector.tensor_scalar(o[0], x[0], a1, a2, f0, f1), [o], ins)

    def act(o, x, f):
        op("a", lambda: g.scalar.activation(o[0], x[0], f), [o], [x])

    def cp(q, o, x):
        if q == "v":
            op("v", lambda: g.vector.tensor_copy(o[0], x[0]), [o], [x])
        else:
            act(o, x, F.Copy)

    def iota(o, pat, base, cm, flag=True):
        if flag:
            op("g", lambda: g.iota(o[0], pat, base, cm, allow_small_or_imprecise_dtypes=True), [o], [])
        else:
            op("g", lambda: g.iota(o[0], pat, base, cm), [o], [])

    def dma(q, o, x):
        op(q, lambda: eng[q].dma_start(o[0], x[0]), [o], [x], kind="dma")

    def hbm(ap):
        return (ap, [])

    def mm(o, l, r):
        op("t", lambda: g.tensor.matmul(o[0], l[0], r[0], True, True), [o], [l, r])

    G8 = slice(0, 8)
    parts = peer_order(T, topo, rank)
    peers = [q for part in parts for q in part]
    runs = []
    for n, q in enumerate(peers + [rank]):
        if runs and q == runs[-1][1] + runs[-1][2] and q != rank:
            runs[-1][2] += 1
        else:
            runs.append([n, q, 1])

    dma("y", vw("tabi", 0, 128), hbm(T.ends[:]))
    dma("a", vw("tabi", 160, 192), hbm(T.bord[:]))
    dma("a", vw("tabi", 128, 160), hbm(T.watch[:]))
    for p in range(D):
        dma("y", vw("posb", p * V, (p + 1) * V), hbm(T.pos[:, p * V:(p + 1) * V]))
    dma("a", vw("kk", 0, 1024, rows=G8), hbm(T.stiff[:]))
    dma("a", vw("kk", 1024, 2048, rows=G8), hbm(T.inv[:]))
    dma("a", vw("kk", 2048, 2560, rows=G8), hbm(T.jstiff[:]))
    dma("a", vw("kk", 2560, 3072, rows=G8), hbm(T.jinv[:]))

    def widen(p):
        o = vw("win%d" % p, BASE, WW)
        x = vw("posb", p * V, (p + 1) * V)
        if CONV[p] == "dma":
            dma("g", o, hbm(T.pos[:, p * V:(p + 1) * V]))
        elif CONV[p] == "g":
            op("g", lambda: g.affine_select(o[0], x[0], [[0, V]], A.is_ge, 0.0, 0, 0), [o], [x])
        else:
            cp(CONV[p], o, x)

    def swap():
        near, half = T.cores[peers[0]], 3 * J // 2
        mine, theirs = (0, 1) if core < near else (1, 0)
        x = vw("fac", 3 * S * CL + half * mine, 3 * S * CL + half * (mine + 1))
        iota(x, [[0, J // 2], [1, 3]], 0, 0)
        n = len(topo.engines(core, near))
        rid, pid = topo.addr(near)[:2]
        op("g", lambda: g.remote_dma(x[0], x[0], T.sem.swap, T.sem.left, pid, rid, topo.mask(core, near)), [], [x],
           kind="remote", sem=("left", n))
        op(None, None, [vw("fac", 3 * S * CL + half * theirs, 3 * S * CL + half * (theirs + 1))], [], kind="arr", sem=("swap", n))

    def values(c):
        iota(vw("val", 512 * c, 512 * (c + 1)), [[1, 512]], PAD + 512 * c, 0)

    iota(vw("pi", 0, 1), [[0, 1]], 0, 1, False)
    iota(vw("pi", 1, 2), [[0, 1]], 0, 17, False)
    iota(vw("coli", 0, 12), [[32, 6], [8, 2]], 0, 0)
    values(0)
    sel = vw("sel", 0, 256, rows=G8)
    iota(sel, [[-2, 2], [0, 128]], 1, 0)
    op("g", lambda: g.affine_select(sel[0], sel[0], [[0, 2], [-1, 8], [0, 16]], A.is_equal, 0.0, 0, 1), [sel], [sel])
    for name in GP:
        if name[0] == "C":
            widen(int(name[1]))
        elif name[0] == "f":
            for k in (0, 1):
                iota(vw("fac", 3 * S * int(name[1]) + k, 3 * S * (int(name[1]) + 1), 3), [[0, S]], k, 0)
        elif name[0] == "v":
            values(int(name[1]))
        elif name == "swap":
            swap()
        else:
            iota(vw("colj", 0, 28), [[16, 28]], RJ, 0)

    kbank = ["px0", "px1", "px2", "p3"]

    def third(name, c):
        return vw(name, 3 * S * c + 2, 3 * (S * c + (S if c < CL else J)), 3)

    def kcopy(c):
        plus, minus = vw("sel", 0, 128, rows=G8), vw("sel", 128, 256, rows=G8)
        if c < CL:
            mm(vw(kbank[c], 0, S), plus, vw("kk", c * S, (c + 1) * S, rows=G8))
            mm(vw(kbank[c], S, 2 * S), minus, vw("kk", 1024 + c * S, 1024 + (c + 1) * S, rows=G8))
        else:
            for n, q, k in runs[:-1]:
                mm(vw("p3", n * B, (n + k) * B), plus, vw("kk", 2048 + q * B, 2048 + (q + k) * B, rows=G8))
                mm(vw("p4", n * B, (n + k) * B), minus, vw("kk", 2560 + q * B, 2560 + (q + k) * B, rows=G8))
        cp("a", third("slot", c), vw(kbank[c], 0, S) if c < CL else vw("p3", 0, J))

    def kw(c):
        tt(third("fac", c), third("slot", c), vw(kbank[c], S, 2 * S) if c < CL else vw("p4", 0, J), A.mult)

    loc = vw("loc", 0, V)

    def fill():
        op("v", lambda: g.vector.memset(loc[0], 8192.0), [loc], [])
        for a in (0, 208):
            o = vw("tabf", a, a + 16)
            op("v", lambda o=o: g.vector.memset(o[0], float(BASE)), [o], [])

    def const():
        p, p17 = vw("pi", 0, 1), vw("pi", 1, 2)
        ts(vw("pj", 0, 1), p, 1, 7, A.logical_shift_right, A.bitwise_and)
        ts(vw("pj", 1, 2), p, 1, None, A.bitwise_and)
        ts(vw("pj", 2, 3), p17, 4, 1, A.logical_shift_right, A.bitwise_and)
        ts(vw("pj", 3, 4), p, 15, None, A.bitwise_and)
        cp("v", vw("pf", 0, 4), vw("pj", 0, 4))
        ts(vw("pf", 4, 5), vw("pf", 2, 3), 208.0, vw("pf", 0, 1), A.mult, A.add)
        ts(vw("pf", 5, 6), vw("pf", 1, 2), 16.0, vw("pf", 4, 5), A.mult, A.add)
        ts(vw("cl", 0, 12), vw("coli", 0, 12), vw("pf", 5, 6), None, A.add)

    def tab():
        ts(vw("tabf", 16, 176), vw("tabi", 0, 160), float(BASE), None, A.add)
        for n, q, k in runs:
            ts(vw("tabf", 176 + 4 * n, 176 + 4 * (n + k)), vw("tabi", 160 + 4 * q, 160 + 4 * (q + k)), float(BASE), None, A.add)

    def transposed():
        for o, x in ((vw("tt", 0, 192), vw("tabf", 16, 208)), (vw("tt", 192, 416), vw("tabf", 0, 224))):
            op("v", lambda o=o, x=x: g.vector.transpose(o[0], x[0]), [o], [x])
        ts(vw("ll", 0, 192), ind(vw("tt", 0, 416), vw("cl", 0, 12)), float(-BASE), None, A.add)

    def scatter(c, q):
        n = 2 * S if c < CL else J
        o = ind(loc, vw("ul", 32 * c, 32 * c + n // 16))
        if q == "a":
            act(o, vw("val", 512 * c, 512 * c + n), F.Silu)
        else:
            ts(o, vw("val", 0, n), 1.0, float(512 * c), A.mult, A.add)

    def lookup(q, lst, seg, w):
        cp(q, vw("rb", 512 * seg, 512 * (seg + 1)), ind(loc, vw("ll", 32 * lst, 32 * (lst + 1))))
        dma("y", vw("wraw", 32 * w, 32 * (w + 1)), vw("rb", 512 * seg, 512 * (seg + 1), rows=slice(0, 128, 16)))

    def tabl(lst):
        return vw("tabf", 16 + 32 * lst, 48 + 32 * lst)

    def finish(last, key):
        if key in "1234" and last.isupper():
            w = int(key) - 1
            k, raw, other = 32, vw("wraw", 32 * w, 32 * w + 32), tabl(5 if w == 3 else w + 1)
        else:
            w, k, raw, other = {"0": (4, 32, vw("wraw", 128, 160), tabl(0)), "1": (5, 96, vw("wraw", 160, 256), vw("wmin", 0, 96)),
                                "w": (8, 32, vw("wraw", 256, 288), tabl(4)), "j": (9, 28, vw("wmin", 96, 124), vw("colj", 32, 60))}[key]
        if last in "Mm":
            tt(vw("wmin", 32 * w, 32 * w + k), raw, other, A.min)
        else:
            ts(vw("ls", 32 * w, 32 * w + k), vw("wmin", 32 * w, 32 * w + k), 0.25, None, A.add)

    def lists(t):
        return ("ul", 0) if t == 0 else ("ls", 32 * {9: 9, 10: 8}.get(t, t - 1))

    def window(t, p):
        return vw("posb", p * V, (p + 1) * V) if t == 0 else vw("win%d" % p, 0, WW)

    def zgather(t, p, q):
        nm, c0 = lists(t)
        cp(q, vw("zb", p * S, (p + 1) * S), ind(window(t, p), vw(nm, c0 + 16, c0 + 32)))

    def task(name):
        if name in ("fill", "const", "tab", "L"):
            {"fill": fill, "const": const, "tab": tab, "L": transposed}[name]()
        elif name == "U":
            cp("v", vw("ul", 0, 128), vw("tabi", 0, 128))
        elif name == "UJ":
            ts(vw("ul", 128, 160), tabl(5), float(-BASE), None, A.add)
        elif name == "cj":
            ts(vw("colj", 32, 60), vw("colj", 0, 28), vw("pf", 3, 4), None, A.add)
        elif name[0] == "S":
            scatter(int(name[1]), name[2])
        elif name[0] == "Z":
            zgather(0, int(name[1]), name[2])
        elif name[0] == "C":
            widen(int(name[1]))
        elif name[:2] == "kw":
            kw(int(name[2]))
        elif name[0] == "k":
            kcopy(int(name[1]))
        elif name[0] == "R":
            w = int(name[1]) - 1
            lookup(name[2], 5 if w == 3 else w + 1, w, w)
        elif name[0] == "r":
            lookup(name[2], int(name[1]), int(name[1]), 4 + int(name[1]))
        else:
            finish(name[0], name[1])

    def plan(t, where):
        for name in PLAN.get((t, where), []):
            task(name)

    def coefficient(off, n, s0, t):
        tt(vw("slot", 3 * s0, 3 * (s0 + n), 3), vw("pa", off, off + n), vw("sq1", off, off + n), A.add)
        plan(t, "v0")
        plan(t, "a0")
        o, f, x = vw("ub", 3 * off, 3 * (off + n)), vw("fac", 3 * s0, 3 * (s0 + n)), vw("slot", 3 * s0, 3 * (s0 + n))
        op("v", lambda: g.vector.tensor_tensor_scan(o[0], f[0], x[0], 0.0, A.mult, A.add), [o], [f, x])
        plan(t, "v1")
        ts(vw("pb", off, off + n), vw("ub", 3 * off + 2, 3 * (off + n), 3), -0.25, 0.25, A.max, A.min)
        plan(t, "v2")
        return [vw("db", p * J + off, p * J + off + n) for p in range(D)]

    def square(p, off, n, s0):
        o = (vw("pa", off, off + n), vw("sq1", off, off + n), vw("slot", 3 * s0 + 1, 3 * (s0 + n), 3))[p]
        act(o, vw("db", p * J + off, p * J + off + n), F.Square)

    def own(t):
        c = t % 5
        nm, c0 = lists(t)
        for p in range(D):
            tt(vw("db", p * J, p * J + S), ind(window(t, p), vw(nm, c0, c0 + 16)), vw("zb", p * S, (p + 1) * S), A.subtract)
            square(p, 0, S, c * S)
        dv = coefficient(0, S, c * S, t)
        for p in range(D):
            cp("a", vw("xb", p * S, (p + 1) * S), ind(window(t, p), vw(nm, c0, c0 + 16)))
        plan(t, "a1")
        mv = [vw("pb", S, 2 * S), vw("pc", 0, S), vw("pc", S, 2 * S)]
        cv, r0 = vw("pb", 0, S), PAD + 2 * S * c

        def move(p):
            tt(vw("win%d" % p, r0, r0 + S), vw("xb", p * S, (p + 1) * S), mv[p], A.add)
            tt(vw("win%d" % p, r0 + S, r0 + 2 * S), vw("zb", p * S, (p + 1) * S), mv[p], A.subtract)
        tt(mv[0], dv[0], cv, A.mult)
        tt(mv[1], dv[1], cv, A.mult)
        move(0)
        plan(t, "v3")
        tt(mv[2], dv[2], cv, A.mult)
        move(1)
        plan(t, "v4")
        move(2)

    off_eng = topo.engines(core, T.cores[parts[-1][0]])
    sent = [0]

    def joint(t):
        w = t // 5
        nm, c0 = lists(t)
        snd, land = "snd%d" % w, "land%d" % w
        cuts = [0]
        for part in parts:
            cuts.append(cuts[-1] + B * len(part))

        def border(q, p, a, b):
            cp(q, vw(snd, D * a + p, D * b, D), ind(window(t, p), vw(nm, c0 + a // 16, c0 + b // 16)))
        border("a", 0, 0, J)
        border("a", 1, 0, J)
        for k in range(len(parts)):
            border("va"[k % 2], 2, cuts[k], cuts[k + 1])
        for k, part in enumerate(parts):
            far = [q for q in part if topo.chip(T.cores[q]) != topo.chip(core)]
            share = len(off_eng) // len(far)
            trs, count = [], 0
            for q in part:
                dst = T.cores[q]
                if q in far:
                    es = off_eng[far.index(q) * share:(far.index(q) + 1) * share]
                else:
                    es = [e for e in topo.engines(core, dst) if e not in off_eng]
                theirs = peer_order(T, topo, q)
                n2 = [x for pt in theirs for x in pt].index(rank)
                k2 = [rank in pt for pt in theirs].index(True)
                n1 = peers.index(q)
                rid, pid = topo.addr(dst)[:2]
                trs.append(RemoteDMATransfer(dst_ids=[DstId(rid=rid, pnc=pid)], dma_engine_mask=sum(1 << e for e in es),
                                             remote_sem=T.sem["arr%d" % (3 * w + k2)],
                                             src=T[snd][:, D * B * n1:D * B * (n1 + 1)], dst=T[land][:, D * B * n2:D * B * (n2 + 1)]))
                count += len(es)
            sent[0] += count
            op("g", lambda trs=trs: g.remote_dma_fused(trs, local_sem=T.sem.sent), [], [vw(snd, D * cuts[k], D * cuts[k + 1])], kind="remote")
            op(None, None, [vw(land, D * cuts[k], D * cuts[k + 1])], [], kind="arr", sem=("arr%d" % (3 * w + k), count))
        plan(t, "s")
        for p in range(D):
            cp("a", vw("px%d" % p, 0, J), vw(snd, p, D * J, D))
        plan(t, "k")
        for k in range(len(parts)):
            a, n = cuts[k], cuts[k + 1] - cuts[k]
            for p in range(D):
                tt(vw("db", p * J + a, p * J + a + n), vw("px%d" % p, a, a + n), vw(land, D * a + p, D * (a + n), D), A.subtract)
                square(p, a, n, CL * S + a)
            dv = coefficient(a, n, CL * S + a, (t, k))
            mv = [vw("mb", p * J + a, p * J + a + n) for p in range(D)]
            cv = vw("pb", a, a + n)

            def move(p):
                tt(vw("win%d" % p, RJ + a, RJ + a + n), vw("px%d" % p, a, a + n), mv[p], A.add)
            tt(mv[0], dv[0], cv, A.mult)
            tt(mv[1], dv[1], cv, A.mult)
            move(0)
            tt(mv[2], dv[2], cv, A.mult)
            move(1)
            move(2)

    for name in PRE:
        task(name)
    for t in range(10):
        if t % 5 == 4:
            joint(t)
        else:
            if t > 0:
                for p in range(D):
                    zgather(t, p, "a")
            own(t)
    nm, c0 = lists(10)

    def watched(q, p, a, b):
        cp(q, vw("yb", p * M + a, p * M + b), ind(window(10, p), vw(nm, c0 + a // 16, c0 + b // 16)))
    watched("a", 0, 0, M)
    watched("v", 1, 0, M)
    watched("a", 2, 0, 384)
    watched("v", 2, 384, M)
    stores = []
    for p in range(D):
        stores.append(len(ops))
        dma("y", hbm(T.y[:, p * M:(p + 1) * M]), vw("yb", p * M, (p + 1) * M))
    ops.append({"q": "y", "fn": None, "deps": set(stores), "kind": "end", "sem": None})

    known = {q: 0 for q in eng}
    at, waits, needed = [], [], set()
    for i, o in enumerate(ops):
        ws = []
        if o["q"] is not None:
            for j in sorted(o["deps"], reverse=True):
                if not known[o["q"]] >> j & 1:
                    ws.append(j)
                    needed.add(j)
                    known[o["q"]] |= at[j] | (1 << j)
        at.append(known[o["q"]] if o["q"] is not None else 0)
        waits.append(ws)
    pool = {q: [] for q in POOLS}
    for i, o in enumerate(ops):
        if i not in needed or o["sem"] is not None:
            continue
        if o["kind"] == "dma":
            q = "s" if o["q"] == "g" else "h"
            pool[q].append([i, 16])
            o["sem"], o["inc"] = (q + str(len(pool[q]) - 1), 16), 16
            continue
        q = o["q"]
        free = [k for k, (last, cnt) in enumerate(pool[q]) if at[i] >> last & 1]
        if free:
            k = min(free, key=lambda k: pool[q][k][0])
        else:
            k = len(pool[q])
            pool[q].append([i, 0])
        pool[q][k] = [i, pool[q][k][1] + 1]
        o["sem"], o["inc"] = (q + str(k), pool[q][k][1]), 1
    for i, o in enumerate(ops):
        for j in waits[i]:
            eng[o["q"]].wait_ge(T.sem[ops[j]["sem"][0]], ops[j]["sem"][1])
        if o["fn"] is not None:
            ins = o["fn"]()
            if "inc" in o:
                ins.then_inc(T.sem[o["sem"][0]], o["inc"])
    g.wait_ge(T.sem.sent, sent[0])
